import numpy as np
import ml_dtypes


def mxq(x, axis, fmt="e4m3"):
    dtype, down = {"e4m3": (ml_dtypes.float8_e4m3fn, 7), "e5m2": (ml_dtypes.float8_e5m2, 14)}[fmt]
    v = np.moveaxis(np.asarray(x, np.float32).astype(ml_dtypes.bfloat16).astype(np.float64), axis, -1)
    blocks = v.reshape(v.shape[:-1] + (-1, 32))
    amax = np.abs(blocks).max(-1, keepdims=True)
    byte = np.maximum(np.where(amax > 0, np.frexp(amax)[1] - 1 + 127, 0) - down, 1)
    scale = np.exp2(byte - 127.0)
    codes = (blocks / scale).astype(np.float32).astype(dtype).astype(np.float64)
    return np.moveaxis((codes * scale).reshape(v.shape), -1, axis)


WIDE = False


def mx_kscale(k):
    if not WIDE:
        return np.ones(k)
    levels = np.array([10, -10, 5, -5, 0])
    if k % 512:
        return np.exp2(np.random.permutation(np.resize(levels, k // 32))).repeat(32)
    a = np.empty((k // 512, 16))
    for p in range(k // 512):
        a[p, :8] = np.random.permutation(np.resize(levels, 8))
        for g in range(8):
            far = levels[np.abs(levels - a[p, g]) >= 10]
            a[p, g + 8] = far[np.random.randint(len(far))]
    return np.exp2(a.ravel()).repeat(32)


def f64(x):
    return np.asarray(x).astype(np.float64)


def striped(idx):
    return np.tile(idx.reshape(-1, 16).T, (8, 1)).astype(np.uint16)


def unstriped(offs):
    return offs[:16].T.reshape(-1).astype(np.int64)


def pack_weight(w):
    k, n = w.shape
    w = f64(np.asarray(w, np.float32).astype(ml_dtypes.bfloat16)).reshape(k // 32, 32, n)
    amax = np.abs(w).max(1)
    byte = np.clip(np.where(amax > 0, np.frexp(amax)[1] - 1 + 127 - 7, 1), 1, 254)
    scaled = (w * np.exp2(127.0 - byte)[:, None, :]).reshape(k, n).astype(np.float32)
    words = np.ascontiguousarray(scaled.reshape(k // 512, 128, 4, n).transpose(0, 1, 3, 2)).astype(ml_dtypes.float8_e4m3fn).view(np.uint8)
    return words, np.ascontiguousarray(byte.astype(np.uint8).reshape(k // 512, 16, n))


def unpack_weight(words, scales):
    g, p, n, _ = words.shape
    vals = np.ascontiguousarray(words).view(ml_dtypes.float8_e4m3fn).astype(np.float64) * np.repeat(np.exp2(scales.astype(np.float64) - 127.0), 8, axis=1)[..., None]
    return vals.transpose(0, 1, 3, 2).reshape(g * 512, n)


def planes(y):
    n, m = y.shape
    v = y.astype(np.float32).astype(ml_dtypes.bfloat16).astype(np.float64).reshape(n // 32, 32, m)
    top = np.abs(v).max(1)
    byte = np.clip(np.where(top > 0, np.frexp(top)[1] - 1 + 127 - 7, 1), 1, 254)
    codes = (v * np.exp2(127.0 - byte)[:, None, :]).reshape(n, m).astype(np.float32).astype(ml_dtypes.float8_e4m3fn).view(np.uint8)
    words = codes.reshape(n // 512, 128, 4, m).transpose(0, 1, 3, 2)
    return np.ascontiguousarray(words), np.ascontiguousarray(byte.astype(np.uint8).reshape(n // 512, 16, m))


K, T, S, H, N = 1024, 1024, 512, 512, 512
P = 2 ** 7


def setup_inputs():
    n = np.random.standard_normal
    s = mx_kscale(K)[:, None]
    u = mx_kscale(H)
    packed_xT = pack_weight(n((K, T)) * s)
    return {
        "x_words": packed_xT[0],
        "x_scales": packed_xT[1],
        "w1": (n((K, H)) / np.sqrt(2 * K) / s * u).astype(np.float32),
        "w2": (n((K, H)) / np.sqrt(2 * K) / s * u).astype(np.float32),
        "w3": (n((H, N)) / np.sqrt(H) / u[:, None]).astype(np.float32),
        "bias": (0.5 * n((H, 1)) * u[:, None]).astype(np.float32),
        "base": (n((N, T))).astype(np.float32),
        "lam": (np.tile(np.random.uniform(0.3, 1.0, S), (P, 1))).astype(np.float32),
        "offs": striped(np.random.permutation(T)[:S]),
    }


def reference(x_words, x_scales, w1, w2, w3, bias, base, lam, offs):
    xq = unpack_weight(x_words, x_scales)[:, unstriped(offs)]
    y = mxq(f64(w2), 0, "e4m3").T @ xq
    dd = (mxq(f64(w1), 0, "e4m3").T @ xq) - y + f64(bias)
    ed = mxq(f64(w3), 0, "e4m3").T @ mxq(dd, 0, "e4m3")
    out = f64(base).copy()
    out[:, unstriped(offs)] = f64(base)[:, unstriped(offs)] + ed * f64(lam)[:1]
    out_0 = out
    return (out_0,) + planes(out_0)

@@ -1,0 +1,159 @@
+from contextlib import ExitStack
+
+import concourse.mybir as mybir
+
+K, T, S, H, N = 1024, 1024, 512, 512, 512
+FLOPS = 2 * S * (2 * K * H + H * N)
+
+F32 = mybir.dt.float32
+BF16 = mybir.dt.bfloat16
+I32 = mybir.dt.int32
+U32 = mybir.dt.uint32
+U16 = mybir.dt.uint16
+U8 = mybir.dt.uint8
+FP8X4 = mybir.dt.float8_e4m3fn_x4
+ALU = mybir.AluOpType
+ACT = mybir.ActivationFunctionType
+
+P = 128
+PACK = 4
+K_PASS = P * PACK
+QUADS = 4
+CHUNK = 256
+
+
+def tile_picked_yreft_lin_po_kernel(tc, x_words, x_scales, w1, w2, w3, bias, base, lam, offs, out_0, out_1, out_2):
+    nc = tc.nc
+    with ExitStack() as ctx:
+        keep = ctx.enter_context(tc.tile_pool(name="keep", bufs=1))
+        psum = ctx.enter_context(tc.psum_pool(name="psum", bufs=1))
+
+        def sb(name, shape, dtype):
+            return keep.tile(shape, dtype, name=name, align_bytes=64)
+
+        offsets = keep.tile([P, S // 16], U16, name="offsets")
+        nc.sync.dma_start(offsets[:], offs)
+
+        scale_table = sb("scale_table", [P, T], U8)
+        nc.vector.memset(scale_table[:].bitcast(I32), 0)
+        for q in range(QUADS):
+            nc.scalar.dma_start(out=scale_table[32 * q : 32 * q + 8, :].bitcast(I32), in_=x_scales[:, 4 * q : 4 * q + 4, :].bitcast(I32))
+        bias_sb = sb("bias_sb", [P, PACK], F32)
+        nc.scalar.dma_start(out=bias_sb[:], in_=bias.rearrange("(p t) o -> p (t o)", t=PACK))
+
+        def load_words(o):
+            table = sb(f"word_table{o}", [P, T], I32)
+            nc.sync.dma_start(out=table[:], in_=x_words[o].rearrange("p n r -> p (n r)").bitcast(I32))
+            return table
+
+        def load_weight(name, rows):
+            raw = sb(name, [P, PACK, H], F32)
+            nc.sync.dma_start(out=raw[:], in_=rows.rearrange("(p j) c -> p j c", j=PACK))
+            return raw
+
+        base_rows = base.rearrange("(p t) c -> p t c", t=PACK)
+        out_rows = out_0.rearrange("(p t) c -> p t c", t=PACK)
+
+        def load_base(t):
+            window = sb(f"window{t}", [P, T], F32)
+            nc.sync.dma_start(out=window[:], in_=base_rows[:, t, :])
+            return window
+
+        word_tables = [load_words(0)]
+        raws = [load_weight("w1_raw0", w1[0:K_PASS, :])]
+        word_tables.append(load_words(1))
+        raws.append(load_weight("w1_raw1", w1[K_PASS:K, :]))
+        raws.append(load_weight("w2_raw0", w2[0:K_PASS, :]))
+        raws.append(load_weight("w2_raw1", w2[K_PASS:K, :]))
+        windows = [load_base(0)]
+        w3_raw = load_weight("w3_raw", w3)
+        lam_sb = sb("lam_sb", [P, S], F32)
+        nc.sync.dma_start(out=lam_sb[:], in_=lam)
+        windows.extend(load_base(t) for t in range(1, PACK))
+
+        def gather_words(o):
+            picked = sb(f"x_codes{o}", [P, S], U32)
+            nc.vector.tensor_copy(picked[:], word_tables[o][:].bitcast(U32).indirect(offsets[:]))
+            return picked
+
+        def round_weight(name, raw, sign, split):
+            grouped = sb(name, [P, PACK * H], BF16)
+            dst = grouped[:].rearrange("p (t m j) -> p m t j", t=PACK, j=PACK)
+            src = raw[:].rearrange("p j (m t) -> p m t j", t=PACK)
+            if split > 0:
+                nc.vector.tensor_scalar(dst[:, :split], src[:, :split], sign, None, ALU.mult)
+            if split < P:
+                nc.scalar.activation(dst[:, split:], src[:, split:], ACT.Copy, scale=sign)
+            return grouped
+
+        def quantize(name, grouped, pieces):
+            width = grouped.shape[1] // PACK
+            codes = sb(name + "_codes", [P, width], U32)
+            scales = sb(name + "_scales", [P, width], U8)
+            step = width // pieces
+            for a in range(0, width, step):
+                nc.vector.quantize_mx(out=codes[:, a : a + step].bitcast(FP8X4), scales=scales[:, a : a + step], in_=grouped[:, PACK * a : PACK * (a + step)])
+            return codes, scales
+
+        def gather_base(t):
+            picked = sb(f"base_picked{t}", [P, S], F32)
+            nc.vector.tensor_copy(picked[:], windows[t][:].indirect(offsets[:]))
+            return picked
+
+        x_codes = [gather_words(0)]
+        x_scale = sb("x_scale", [P, S], U8)
+        nc.vector.tensor_copy(x_scale[:], scale_table[:].indirect(offsets[:]))
+
+        dd_banks = [psum.tile([P, S], F32, name=f"dd_bank{t}") for t in range(PACK)]
+        passes = [(0, 1.0, 64, 1), (1, 1.0, 64, 1), (0, -1.0, 64, 1), (1, -1.0, 88, 2)]
+        for i, (o, sign, split, pieces) in enumerate(passes):
+            grouped = round_weight(f"w_grouped{i}", raws[i], sign, split)
+            codes, scales = quantize(f"w{i}", grouped, pieces)
+            if i == 0:
+                x_codes.append(gather_words(1))
+            for t in range(PACK):
+                cols = slice(t * P, (t + 1) * P)
+                nc.tensor.matmul_mx(out=dd_banks[t][:], lhsT=codes[:, cols].bitcast(FP8X4), lhsT_scale=scales[:, cols],
+                                    rhs=x_codes[o][:].bitcast(FP8X4), rhs_scale=x_scale[4 * o : P, :],
+                                    start=(i == 0), stop=(i == len(passes) - 1))
+
+        dd_planes = sb("dd_planes", [P, PACK, S], BF16)
+        for t in range(PACK):
+            if t == 1:
+                nc.vector.tensor_scalar(dd_planes[:, t, :], dd_banks[t][:], bias_sb[:, t : t + 1], None, ALU.add)
+            else:
+                nc.scalar.activation(dd_planes[:, t, :], dd_banks[t][:], ACT.Identity, bias=bias_sb[:, t : t + 1])
+        base_picked = [gather_base(0)]
+        dd_grouped = sb("dd_grouped", [P, PACK * S], BF16)
+        nc.vector.tensor_copy(dd_grouped[:].rearrange("p (c i t) -> p c t i", i=4, t=PACK), dd_planes[:].rearrange("p t (c i) -> p c t i", i=4))
+        dd_codes, dd_scales = quantize("dd", dd_grouped, 1)
+
+        w3_grouped = round_weight("w3_grouped", w3_raw, 1.0, 48)
+        w3_codes, w3_scales = quantize("w3", w3_grouped, 1)
+
+        chunks = range(T // CHUNK)
+        out_grouped = [sb(f"out_grouped{c}", [P, CHUNK, PACK], BF16) for c in chunks]
+        for t in range(PACK):
+            cols = slice(t * P, (t + 1) * P)
+            ed_bank = psum.tile([P, S], F32, name=f"ed_bank{t}")
+            nc.tensor.matmul_mx(out=ed_bank[:], lhsT=w3_codes[:, cols].bitcast(FP8X4), lhsT_scale=w3_scales[:, cols],
+                                rhs=dd_codes[:].bitcast(FP8X4), rhs_scale=dd_scales[:], start=True, stop=True)
+            edit = sb(f"edit{t}", [P, S], F32)
+            nc.vector.tensor_tensor(edit[:], ed_bank[:], lam_sb[:], ALU.mult)
+            if t > 0:
+                base_picked.append(gather_base(t))
+            nc.vector.tensor_tensor(windows[t][:].indirect(offsets[:]), edit[:], base_picked[t][:], ALU.add)
+            nc.sync.dma_start(out=out_rows[:, t, :], in_=windows[t][:])
+            for c in chunks:
+                nc.scalar.copy(out_grouped[c][:, :, t], windows[t][:, c * CHUNK : (c + 1) * CHUNK])
+
+        out_scales = sb("out_scales", [P, T], U8)
+        word_rows = out_1[0].rearrange("p n r -> p (n r)").bitcast(I32)
+        for c in chunks:
+            cols = slice(c * CHUNK, (c + 1) * CHUNK)
+            out_codes = sb(f"out_codes{c}", [P, CHUNK], I32)
+            nc.vector.quantize_mx(out=out_codes[:].bitcast(FP8X4), scales=out_scales[:, cols], in_=out_grouped[c][:].rearrange("p c t -> p (c t)"))
+            nc.sync.dma_start(out=word_rows[:, cols], in_=out_codes[:])
+        for q in range(QUADS):
+            queue = nc.scalar if q % 2 else nc.sync
+            queue.dma_start(out=out_2[0, 4 * q : 4 * q + 4, :].bitcast(I32), in_=out_scales[32 * q : 32 * q + 4, :].bitcast(I32))

@@ -1,6 +1,7 @@
 from contextlib import ExitStack
 
 import concourse.mybir as mybir
+from concourse.masks import make_identity
 
 K, T, S, H, N = 1024, 1024, 512, 512, 512
 FLOPS = 2 * S * (2 * K * H + H * N)
@@ -20,6 +21,8 @@ PACK = 4
 K_PASS = P * PACK
 QUADS = 4
 CHUNK = 256
+TAIL_SPLIT = 640
+ORDER = (2, 3, 0, 1)
 
 
 def tile_picked_yreft_lin_po_kernel(tc, x_words, x_scales, w1, w2, w3, bias, base, lam, offs, out_0, out_1, out_2):
@@ -28,8 +31,8 @@ def tile_picked_yreft_lin_po_kernel(tc, x_words, x_scales, w1, w2, w3, bias, bas
         keep = ctx.enter_context(tc.tile_pool(name="keep", bufs=1))
         psum = ctx.enter_context(tc.psum_pool(name="psum", bufs=1))
 
-        def sb(name, shape, dtype):
-            return keep.tile(shape, dtype, name=name, align_bytes=64)
+        def sb(name, shape, dtype, tag=None):
+            return keep.tile(shape, dtype, name=name, tag=tag or name, align_bytes=64)
 
         offsets = keep.tile([P, S // 16], U16, name="offsets")
         nc.sync.dma_start(offsets[:], offs)
@@ -65,11 +68,13 @@ def tile_picked_yreft_lin_po_kernel(tc, x_words, x_scales, w1, w2, w3, bias, bas
         raws.append(load_weight("w1_raw1", w1[K_PASS:K, :]))
         raws.append(load_weight("w2_raw0", w2[0:K_PASS, :]))
         raws.append(load_weight("w2_raw1", w2[K_PASS:K, :]))
-        windows = [load_base(0)]
+        windows = {ORDER[0]: load_base(ORDER[0])}
         w3_raw = load_weight("w3_raw", w3)
+        windows[ORDER[1]] = load_base(ORDER[1])
         lam_sb = sb("lam_sb", [P, S], F32)
         nc.sync.dma_start(out=lam_sb[:], in_=lam)
-        windows.extend(load_base(t) for t in range(1, PACK))
+        for t in ORDER[2:]:
+            windows[t] = load_base(t)
 
         def gather_words(o):
             picked = sb(f"x_codes{o}", [P, S], U32)
@@ -95,8 +100,8 @@ def tile_picked_yreft_lin_po_kernel(tc, x_words, x_scales, w1, w2, w3, bias, bas
                 nc.vector.quantize_mx(out=codes[:, a : a + step].bitcast(FP8X4), scales=scales[:, a : a + step], in_=grouped[:, PACK * a : PACK * (a + step)])
             return codes, scales
 
-        def gather_base(t):
-            picked = sb(f"base_picked{t}", [P, S], F32)
+        def gather_base(t, tag=None):
+            picked = sb(f"base_picked{t}", [P, S], F32, tag)
             nc.vector.tensor_copy(picked[:], windows[t][:].indirect(offsets[:]))
             return picked
 
@@ -104,11 +109,11 @@ def tile_picked_yreft_lin_po_kernel(tc, x_words, x_scales, w1, w2, w3, bias, bas
         x_scale = sb("x_scale", [P, S], U8)
         nc.vector.tensor_copy(x_scale[:], scale_table[:].indirect(offsets[:]))
 
-        dd_banks = [psum.tile([P, S], F32, name=f"dd_bank{t}") for t in range(PACK)]
+        dd_banks = [psum.tile([P, S], F32, name=f"dd_bank{t}", tag=f"bank{t}") for t in range(PACK)]
         passes = [(0, 1.0, 64, 1), (1, 1.0, 64, 1), (0, -1.0, 64, 1), (1, -1.0, 88, 2)]
         for i, (o, sign, split, pieces) in enumerate(passes):
             grouped = round_weight(f"w_grouped{i}", raws[i], sign, split)
-            codes, scales = quantize(f"w{i}", grouped, pieces)
+            codes, scales = quantize(f"w12_{i}", grouped, pieces)
             if i == 0:
                 x_codes.append(gather_words(1))
             for t in range(PACK):
@@ -117,43 +122,94 @@ def tile_picked_yreft_lin_po_kernel(tc, x_words, x_scales, w1, w2, w3, bias, bas
                                     rhs=x_codes[o][:].bitcast(FP8X4), rhs_scale=x_scale[4 * o : P, :],
                                     start=(i == 0), stop=(i == len(passes) - 1))
 
+        first, last = ORDER[0], ORDER[-1]
+        blocks = S // P
+        identity = sb("identity", [P, P], F32)
+        make_identity(nc, identity[:])
+        lam_bank = psum.tile([P, blocks, P], F32, name="lam_bank", tag="bank5")
+        for b in range(blocks):
+            nc.tensor.transpose(lam_bank[:, b, :], lam_sb[:, b * P : (b + 1) * P], identity[:])
+        lam_cols = sb("lam_cols", [P, blocks], F32)
+
         dd_planes = sb("dd_planes", [P, PACK, S], BF16)
         for t in range(PACK):
-            if t == 1:
-                nc.vector.tensor_scalar(dd_planes[:, t, :], dd_banks[t][:], bias_sb[:, t : t + 1], None, ALU.add)
-            else:
-                nc.scalar.activation(dd_planes[:, t, :], dd_banks[t][:], ACT.Identity, bias=bias_sb[:, t : t + 1])
-        base_picked = [gather_base(0)]
-        dd_grouped = sb("dd_grouped", [P, PACK * S], BF16)
-        nc.vector.tensor_copy(dd_grouped[:].rearrange("p (c i t) -> p c t i", i=4, t=PACK), dd_planes[:].rearrange("p t (c i) -> p c t i", i=4))
-        dd_codes, dd_scales = quantize("dd", dd_grouped, 1)
-
-        w3_grouped = round_weight("w3_grouped", w3_raw, 1.0, 48)
+            nc.scalar.activation(dd_planes[:, t, :], dd_banks[t][:], ACT.Identity, bias=bias_sb[:, t : t + 1])
+        base_picked = {first: gather_base(first)}
+        w3_grouped = round_weight("w3_grouped", w3_raw, 1.0, P)
         w3_codes, w3_scales = quantize("w3", w3_grouped, 1)
+        base_picked[ORDER[1]] = gather_base(ORDER[1])
+        dd_grouped = sb("dd_grouped", [P, PACK * S], BF16)
+        dst = dd_grouped[:].rearrange("p (c i t) -> p c t i", i=4, t=PACK)
+        src = dd_planes[:].rearrange("p t (c i) -> p c t i", i=4)
+        nc.scalar.copy(dst[:, :100], src[:, :100])
+        nc.vector.tensor_copy(dst[:, 100:], src[:, 100:])
+        nc.scalar.copy(lam_cols[:], lam_bank[:, :, 0])
+        dd_codes, dd_scales = quantize("dd", dd_grouped, 1)
+        base_picked[ORDER[2]] = gather_base(ORDER[2], "dd_grouped")
 
-        chunks = range(T // CHUNK)
-        out_grouped = [sb(f"out_grouped{c}", [P, CHUNK, PACK], BF16) for c in chunks]
-        for t in range(PACK):
-            cols = slice(t * P, (t + 1) * P)
-            ed_bank = psum.tile([P, S], F32, name=f"ed_bank{t}")
-            nc.tensor.matmul_mx(out=ed_bank[:], lhsT=w3_codes[:, cols].bitcast(FP8X4), lhsT_scale=w3_scales[:, cols],
-                                rhs=dd_codes[:].bitcast(FP8X4), rhs_scale=dd_scales[:], start=True, stop=True)
-            edit = sb(f"edit{t}", [P, S], F32)
-            nc.vector.tensor_tensor(edit[:], ed_bank[:], lam_sb[:], ALU.mult)
-            if t > 0:
-                base_picked.append(gather_base(t))
-            nc.vector.tensor_tensor(windows[t][:].indirect(offsets[:]), edit[:], base_picked[t][:], ALU.add)
+        ed_bank = psum.tile([P, S], F32, name="ed_bank", tag="bank4")
+        nc.tensor.matmul_mx(out=ed_bank[:], lhsT=w3_codes[:, first * P : (first + 1) * P].bitcast(FP8X4), lhsT_scale=w3_scales[:, first * P : (first + 1) * P],
+                            rhs=dd_codes[:].bitcast(FP8X4), rhs_scale=dd_scales[:], start=True, stop=True)
+        edits = {first: sb("edit_first", [P, S], F32)}
+        nc.vector.tensor_tensor(edits[first][:], ed_bank[:], lam_sb[:], ALU.mult)
+
+        base_picked[last] = gather_base(last)
+        turned = sb("turned", [P, blocks, N - P], F32)
+        for b in range(blocks):
+            toks = slice(b * P, (b + 1) * P)
+            bank = psum.tile([P, N - P], F32, name=f"turned_bank{b}", tag=f"bank{b}")
+            for a, z, at in ((3 * P, N, 0), (0, 2 * P, P)):
+                nc.tensor.matmul_mx(out=bank[:, at : at + z - a], lhsT=dd_codes[:, toks].bitcast(FP8X4), lhsT_scale=dd_scales[:, toks],
+                                    rhs=w3_codes[:, a:z].bitcast(FP8X4), rhs_scale=w3_scales[:, a:z], start=True, stop=True)
+            nc.scalar.activation(turned[:, b, :], bank[:], ACT.Copy, scale=lam_cols[:, b : b + 1])
+        back_banks = {}
+        for i, t in enumerate(ORDER[1:]):
+            back_banks[t] = psum.tile([P, S], F32, name=f"back_bank{t}", tag=f"bank{5 + i}")
+            for b in range(blocks):
+                nc.tensor.transpose(back_banks[t][:, b * P : (b + 1) * P], turned[:, b, i * P : (i + 1) * P], identity[:])
+        for t in ORDER[1:]:
+            edits[t] = sb(f"edit{t}", [P, S], F32)
+            nc.scalar.copy(edits[t][:], back_banks[t][:])
+
+        shares = (
+            (nc.vector.tensor_copy, "turned", ((0, 256), (256, 512))),
+            (nc.scalar.copy, "identity", ((512, 768), (768, 896), (896, 1024))),
+        )
+        planes, grouped_out = {}, {}
+        for copy, tag, pieces in shares:
+            a, z = pieces[0][0], pieces[-1][1]
+            planes[a] = sb(f"out_planes{a}", [P, PACK, z - a], BF16, tag)
+            for piece in pieces:
+                grouped_out[piece] = sb(f"out_grouped{piece[0]}", [P, piece[1] - piece[0], PACK], BF16)
+
+        def round_plane(t, copy, pieces):
+            start = pieces[0][0]
+            for a, z in pieces if t == last else ((start, pieces[-1][1]),):
+                copy(planes[start][:, t, a - start : z - start], windows[t][:, a:z])
+
+        def weave_pair(t, copy, pieces):
+            start = pieces[0][0]
+            for a, z in pieces:
+                copy(grouped_out[a, z][:, :, t : t + 2], planes[start][:].rearrange("p t c -> p c t")[:, a - start : z - start, t : t + 2])
+
+        for t in ORDER:
+            nc.vector.tensor_tensor(windows[t][:].indirect(offsets[:]), edits[t][:], base_picked[t][:], ALU.add)
             nc.sync.dma_start(out=out_rows[:, t, :], in_=windows[t][:])
-            for c in chunks:
-                nc.scalar.copy(out_grouped[c][:, :, t], windows[t][:, c * CHUNK : (c + 1) * CHUNK])
+            for copy, tag, pieces in shares:
+                round_plane(t, copy if t == last else nc.scalar.copy, pieces)
+            if t % 2:
+                for copy, tag, pieces in shares:
+                    weave_pair(t - 1, copy if t == last else nc.scalar.copy, pieces)
 
         out_scales = sb("out_scales", [P, T], U8)
         word_rows = out_1[0].rearrange("p n r -> p (n r)").bitcast(I32)
-        for c in chunks:
-            cols = slice(c * CHUNK, (c + 1) * CHUNK)
-            out_codes = sb(f"out_codes{c}", [P, CHUNK], I32)
-            nc.vector.quantize_mx(out=out_codes[:].bitcast(FP8X4), scales=out_scales[:, cols], in_=out_grouped[c][:].rearrange("p c t -> p (c t)"))
-            nc.sync.dma_start(out=word_rows[:, cols], in_=out_codes[:])
+        out_codes = sb("out_codes", [P, T], I32)
+        stored = 0
+        for a, z in grouped_out:
+            nc.vector.quantize_mx(out=out_codes[:, a:z].bitcast(FP8X4), scales=out_scales[:, a:z], in_=grouped_out[a, z][:].rearrange("p c t -> p (c t)"))
+            if z in (512, 768, 1024):
+                nc.sync.dma_start(out=word_rows[:, stored:z], in_=out_codes[:, stored:z])
+                stored = z
         for q in range(QUADS):
             queue = nc.scalar if q % 2 else nc.sync
             queue.dma_start(out=out_2[0, 4 * q : 4 * q + 4, :].bitcast(I32), in_=out_scales[32 * q : 32 * q + 4, :].bitcast(I32))

@@ -34,16 +34,6 @@ def tile_picked_yreft_lin_po_kernel(tc, x_words, x_scales, w1, w2, w3, bias, bas
         def sb(name, shape, dtype, tag=None):
             return keep.tile(shape, dtype, name=name, tag=tag or name, align_bytes=64)
 
-        offsets = keep.tile([P, S // 16], U16, name="offsets")
-        nc.sync.dma_start(offsets[:], offs)
-
-        scale_table = sb("scale_table", [P, T], U8)
-        nc.vector.memset(scale_table[:].bitcast(I32), 0)
-        for q in range(QUADS):
-            nc.scalar.dma_start(out=scale_table[32 * q : 32 * q + 8, :].bitcast(I32), in_=x_scales[:, 4 * q : 4 * q + 4, :].bitcast(I32))
-        bias_sb = sb("bias_sb", [P, PACK], F32)
-        nc.scalar.dma_start(out=bias_sb[:], in_=bias.rearrange("(p t) o -> p (t o)", t=PACK))
-
         def load_words(o):
             table = sb(f"word_table{o}", [P, T], I32)
             nc.sync.dma_start(out=table[:], in_=x_words[o].rearrange("p n r -> p (n r)").bitcast(I32))
@@ -63,10 +53,21 @@ def tile_picked_yreft_lin_po_kernel(tc, x_words, x_scales, w1, w2, w3, bias, bas
             return window
 
         word_tables = [load_words(0)]
+        offsets = keep.tile([P, S // 16], U16, name="offsets")
+        nc.sync.dma_start(offsets[:], offs)
+        scale_table = sb("scale_table", [P, T], U8)
+        nc.gpsimd.memset(scale_table[:].bitcast(I32), 0)
+        scale_rows = sb("scale_rows", [P, T // 4], I32)
+        for q in range(QUADS):
+            rows = slice(32 * q, 32 * q + 8)
+            nc.sync.dma_start(out=scale_rows[rows, :], in_=x_scales[:, 4 * q : 4 * q + 4, :].bitcast(I32))
+            nc.vector.tensor_copy(scale_table[rows, :].bitcast(I32), scale_rows[rows, :])
         raws = [load_weight("w1_raw0", w1[0:K_PASS, :])]
         word_tables.append(load_words(1))
         raws.append(load_weight("w1_raw1", w1[K_PASS:K, :]))
         raws.append(load_weight("w2_raw0", w2[0:K_PASS, :]))
+        bias_sb = sb("bias_sb", [P, PACK], F32)
+        nc.sync.dma_start(out=bias_sb[:], in_=bias.rearrange("(p t) o -> p (t o)", t=PACK))
         raws.append(load_weight("w2_raw1", w2[K_PASS:K, :]))
         windows = {ORDER[0]: load_base(ORDER[0])}
         w3_raw = load_weight("w3_raw", w3)
@@ -110,7 +111,7 @@ def tile_picked_yreft_lin_po_kernel(tc, x_words, x_scales, w1, w2, w3, bias, bas
         nc.vector.tensor_copy(x_scale[:], scale_table[:].indirect(offsets[:]))
 
         dd_banks = [psum.tile([P, S], F32, name=f"dd_bank{t}", tag=f"bank{t}") for t in range(PACK)]
-        passes = [(0, 1.0, 64, 1), (1, 1.0, 64, 1), (0, -1.0, 64, 1), (1, -1.0, 88, 2)]
+        passes = [(0, 1.0, 0, 1), (1, 1.0, 32, 1), (0, -1.0, 32, 1), (1, -1.0, 88, 2)]
         for i, (o, sign, split, pieces) in enumerate(passes):
             grouped = round_weight(f"w_grouped{i}", raws[i], sign, split)
             codes, scales = quantize(f"w12_{i}", grouped, pieces)

@@ -20,12 +20,22 @@ P = 128
 PACK = 4
 K_PASS = P * PACK
 QUADS = 4
-CHUNK = 256
-TAIL_SPLIT = 640
+LIST_ROWS = 16
+BLOCKS = S // P
+
 ORDER = (2, 3, 0, 1)
+FIRST, LAST = ORDER[0], ORDER[-1]
+
+VECTOR_SHARES = (0, 32, 64, 88)
+
+VECTOR_PIECES = ((0, 256), (256, 512))
+SCALAR_PIECES = ((512, 768), (768, 896), (896, 1024))
+WORD_STORES = (512, 768, 1024)
 
 
-def tile_picked_yreft_lin_po_kernel(tc, x_words, x_scales, w1, w2, w3, bias, base, lam, offs, out_0, out_1, out_2):
+def tile_picked_yreft_lin_po_kernel(
+    tc, x_words, x_scales, w1, w2, w3, bias, base, lam, offs, out_0, out_1, out_2
+):
     nc = tc.nc
     with ExitStack() as ctx:
         keep = ctx.enter_context(tc.tile_pool(name="keep", bufs=1))
@@ -33,6 +43,9 @@ def tile_picked_yreft_lin_po_kernel(tc, x_words, x_scales, w1, w2, w3, bias, bas
 
         def sb(name, shape, dtype, tag=None):
             return keep.tile(shape, dtype, name=name, tag=tag or name, align_bytes=64)
+
+        base_slots = base.rearrange("(p t) c -> p t c", t=PACK)
+        out_slots = out_0.rearrange("(p t) c -> p t c", t=PACK)
 
         def load_words(o):
             table = sb(f"word_table{o}", [P, T], I32)
@@ -44,32 +57,31 @@ def tile_picked_yreft_lin_po_kernel(tc, x_words, x_scales, w1, w2, w3, bias, bas
             nc.sync.dma_start(out=raw[:], in_=rows.rearrange("(p j) c -> p j c", j=PACK))
             return raw
 
-        base_rows = base.rearrange("(p t) c -> p t c", t=PACK)
-        out_rows = out_0.rearrange("(p t) c -> p t c", t=PACK)
-
         def load_base(t):
             window = sb(f"window{t}", [P, T], F32)
-            nc.sync.dma_start(out=window[:], in_=base_rows[:, t, :])
+            nc.sync.dma_start(out=window[:], in_=base_slots[:, t, :])
             return window
 
         word_tables = [load_words(0)]
-        offsets = keep.tile([P, S // 16], U16, name="offsets")
+        offsets = keep.tile([P, S // LIST_ROWS], U16, name="offsets")
         nc.sync.dma_start(offsets[:], offs)
+
         scale_table = sb("scale_table", [P, T], U8)
         nc.gpsimd.memset(scale_table[:].bitcast(I32), 0)
         scale_rows = sb("scale_rows", [P, T // 4], I32)
         for q in range(QUADS):
-            rows = slice(32 * q, 32 * q + 8)
-            nc.sync.dma_start(out=scale_rows[rows, :], in_=x_scales[:, 4 * q : 4 * q + 4, :].bitcast(I32))
-            nc.vector.tensor_copy(scale_table[rows, :].bitcast(I32), scale_rows[rows, :])
-        raws = [load_weight("w1_raw0", w1[0:K_PASS, :])]
+            live = slice(32 * q, 32 * q + 8)
+            nc.sync.dma_start(out=scale_rows[live, :], in_=x_scales[:, 4 * q : 4 * q + 4, :].bitcast(I32))
+            nc.vector.tensor_copy(scale_table[live, :].bitcast(I32), scale_rows[live, :])
+
+        w12_raw = [load_weight("w1_raw0", w1[0:K_PASS, :])]
         word_tables.append(load_words(1))
-        raws.append(load_weight("w1_raw1", w1[K_PASS:K, :]))
-        raws.append(load_weight("w2_raw0", w2[0:K_PASS, :]))
+        w12_raw.append(load_weight("w1_raw1", w1[K_PASS:K, :]))
+        w12_raw.append(load_weight("w2_raw0", w2[0:K_PASS, :]))
         bias_sb = sb("bias_sb", [P, PACK], F32)
         nc.sync.dma_start(out=bias_sb[:], in_=bias.rearrange("(p t) o -> p (t o)", t=PACK))
-        raws.append(load_weight("w2_raw1", w2[K_PASS:K, :]))
-        windows = {ORDER[0]: load_base(ORDER[0])}
+        w12_raw.append(load_weight("w2_raw1", w2[K_PASS:K, :]))
+        windows = {FIRST: load_base(FIRST)}
         w3_raw = load_weight("w3_raw", w3)
         windows[ORDER[1]] = load_base(ORDER[1])
         lam_sb = sb("lam_sb", [P, S], F32)
@@ -82,135 +94,157 @@ def tile_picked_yreft_lin_po_kernel(tc, x_words, x_scales, w1, w2, w3, bias, bas
             nc.vector.tensor_copy(picked[:], word_tables[o][:].bitcast(U32).indirect(offsets[:]))
             return picked
 
-        def round_weight(name, raw, sign, split):
-            grouped = sb(name, [P, PACK * H], BF16)
-            dst = grouped[:].rearrange("p (t m j) -> p m t j", t=PACK, j=PACK)
-            src = raw[:].rearrange("p j (m t) -> p m t j", t=PACK)
-            if split > 0:
-                nc.vector.tensor_scalar(dst[:, :split], src[:, :split], sign, None, ALU.mult)
-            if split < P:
-                nc.scalar.activation(dst[:, split:], src[:, split:], ACT.Copy, scale=sign)
-            return grouped
-
-        def quantize(name, grouped, pieces):
-            width = grouped.shape[1] // PACK
-            codes = sb(name + "_codes", [P, width], U32)
-            scales = sb(name + "_scales", [P, width], U8)
-            step = width // pieces
-            for a in range(0, width, step):
-                nc.vector.quantize_mx(out=codes[:, a : a + step].bitcast(FP8X4), scales=scales[:, a : a + step], in_=grouped[:, PACK * a : PACK * (a + step)])
-            return codes, scales
-
         def gather_base(t, tag=None):
             picked = sb(f"base_picked{t}", [P, S], F32, tag)
             nc.vector.tensor_copy(picked[:], windows[t][:].indirect(offsets[:]))
             return picked
+
+        def round_weight(name, raw, sign, vector_share):
+            grouped = sb(name, [P, PACK * H], BF16)
+            dealt = grouped[:].rearrange("p (t m j) -> p m t j", t=PACK, j=PACK)
+            plain = raw[:].rearrange("p j (m t) -> p m t j", t=PACK)
+            if vector_share > 0:
+                nc.vector.tensor_scalar(dealt[:, :vector_share], plain[:, :vector_share], sign, None, ALU.mult)
+            if vector_share < P:
+                nc.scalar.activation(dealt[:, vector_share:], plain[:, vector_share:], ACT.Copy, scale=sign)
+            return grouped
+
+        def quantize(name, grouped, calls):
+            width = grouped.shape[1] // PACK
+            codes = sb(name + "_codes", [P, width], U32)
+            scales = sb(name + "_scales", [P, width], U8)
+            step = width // calls
+            for a in range(0, width, step):
+                nc.vector.quantize_mx(
+                    out=codes[:, a : a + step].bitcast(FP8X4),
+                    scales=scales[:, a : a + step],
+                    in_=grouped[:, PACK * a : PACK * (a + step)],
+                )
+            return codes, scales
+
+        def product(out, left, left_scales, right, right_scales, start=True, stop=True):
+            nc.tensor.matmul_mx(
+                out=out,
+                lhsT=left.bitcast(FP8X4),
+                lhsT_scale=left_scales,
+                rhs=right.bitcast(FP8X4),
+                rhs_scale=right_scales,
+                start=start,
+                stop=stop,
+            )
 
         x_codes = [gather_words(0)]
         x_scale = sb("x_scale", [P, S], U8)
         nc.vector.tensor_copy(x_scale[:], scale_table[:].indirect(offsets[:]))
 
         dd_banks = [psum.tile([P, S], F32, name=f"dd_bank{t}", tag=f"bank{t}") for t in range(PACK)]
-        passes = [(0, 1.0, 0, 1), (1, 1.0, 32, 1), (0, -1.0, 32, 1), (1, -1.0, 88, 2)]
-        for i, (o, sign, split, pieces) in enumerate(passes):
-            grouped = round_weight(f"w_grouped{i}", raws[i], sign, split)
-            codes, scales = quantize(f"w12_{i}", grouped, pieces)
+        passes = [(sign, o) for sign in (1.0, -1.0) for o in range(K // K_PASS)]
+        for i, (sign, o) in enumerate(passes):
+            closing = i == len(passes) - 1
+            grouped = round_weight(f"w12_grouped{i}", w12_raw[i], sign, VECTOR_SHARES[i])
+            codes, scales = quantize(f"w12_{i}", grouped, 2 if closing else 1)
             if i == 0:
                 x_codes.append(gather_words(1))
             for t in range(PACK):
-                cols = slice(t * P, (t + 1) * P)
-                nc.tensor.matmul_mx(out=dd_banks[t][:], lhsT=codes[:, cols].bitcast(FP8X4), lhsT_scale=scales[:, cols],
-                                    rhs=x_codes[o][:].bitcast(FP8X4), rhs_scale=x_scale[4 * o : P, :],
-                                    start=(i == 0), stop=(i == len(passes) - 1))
+                slot = slice(t * P, (t + 1) * P)
+                product(dd_banks[t][:], codes[:, slot], scales[:, slot], x_codes[o][:], x_scale[4 * o : P, :],
+                        start=(i == 0), stop=closing)
 
-        first, last = ORDER[0], ORDER[-1]
-        blocks = S // P
         identity = sb("identity", [P, P], F32)
         make_identity(nc, identity[:])
-        lam_bank = psum.tile([P, blocks, P], F32, name="lam_bank", tag="bank5")
-        for b in range(blocks):
+        lam_bank = psum.tile([P, BLOCKS, P], F32, name="lam_bank", tag="bank5")
+        for b in range(BLOCKS):
             nc.tensor.transpose(lam_bank[:, b, :], lam_sb[:, b * P : (b + 1) * P], identity[:])
-        lam_cols = sb("lam_cols", [P, blocks], F32)
+        lam_cols = sb("lam_cols", [P, BLOCKS], F32)
 
-        dd_planes = sb("dd_planes", [P, PACK, S], BF16)
-        for t in range(PACK):
-            nc.scalar.activation(dd_planes[:, t, :], dd_banks[t][:], ACT.Identity, bias=bias_sb[:, t : t + 1])
-        base_picked = {first: gather_base(first)}
+        dd_slots = sb("dd_slots", [P, PACK, S], BF16)
+        base_picked = {FIRST: gather_base(FIRST)}
+        for t in range(PACK - 1):
+            nc.scalar.activation(dd_slots[:, t, :], dd_banks[t][:], ACT.Identity, bias=bias_sb[:, t : t + 1])
+        nc.vector.tensor_scalar(dd_slots[:, PACK - 1, :], dd_banks[PACK - 1][:], bias_sb[:, PACK - 1 :], None, ALU.add)
         w3_grouped = round_weight("w3_grouped", w3_raw, 1.0, P)
-        w3_codes, w3_scales = quantize("w3", w3_grouped, 1)
         base_picked[ORDER[1]] = gather_base(ORDER[1])
+        w3_codes, w3_scales = quantize("w3", w3_grouped, 1)
         dd_grouped = sb("dd_grouped", [P, PACK * S], BF16)
-        dst = dd_grouped[:].rearrange("p (c i t) -> p c t i", i=4, t=PACK)
-        src = dd_planes[:].rearrange("p t (c i) -> p c t i", i=4)
-        nc.scalar.copy(dst[:, :100], src[:, :100])
-        nc.vector.tensor_copy(dst[:, 100:], src[:, 100:])
+        nc.scalar.copy(
+            dd_grouped[:].rearrange("p (c i t) -> p c t i", i=4, t=PACK),
+            dd_slots[:].rearrange("p t (c i) -> p c t i", i=4),
+        )
         nc.scalar.copy(lam_cols[:], lam_bank[:, :, 0])
         dd_codes, dd_scales = quantize("dd", dd_grouped, 1)
         base_picked[ORDER[2]] = gather_base(ORDER[2], "dd_grouped")
 
+        edits = {FIRST: sb("edit_first", [P, S], F32)}
         ed_bank = psum.tile([P, S], F32, name="ed_bank", tag="bank4")
-        nc.tensor.matmul_mx(out=ed_bank[:], lhsT=w3_codes[:, first * P : (first + 1) * P].bitcast(FP8X4), lhsT_scale=w3_scales[:, first * P : (first + 1) * P],
-                            rhs=dd_codes[:].bitcast(FP8X4), rhs_scale=dd_scales[:], start=True, stop=True)
-        edits = {first: sb("edit_first", [P, S], F32)}
-        nc.vector.tensor_tensor(edits[first][:], ed_bank[:], lam_sb[:], ALU.mult)
+        slot = slice(FIRST * P, (FIRST + 1) * P)
+        product(ed_bank[:], w3_codes[:, slot], w3_scales[:, slot], dd_codes[:], dd_scales[:])
+        nc.vector.tensor_tensor(edits[FIRST][:], ed_bank[:], lam_sb[:], ALU.mult)
+        base_picked[LAST] = gather_base(LAST)
 
-        base_picked[last] = gather_base(last)
-        turned = sb("turned", [P, blocks, N - P], F32)
-        for b in range(blocks):
-            toks = slice(b * P, (b + 1) * P)
+        turned = sb("turned", [P, BLOCKS, N - P], F32)
+        for b in range(BLOCKS):
+            entries = slice(b * P, (b + 1) * P)
             bank = psum.tile([P, N - P], F32, name=f"turned_bank{b}", tag=f"bank{b}")
-            for a, z, at in ((3 * P, N, 0), (0, 2 * P, P)):
-                nc.tensor.matmul_mx(out=bank[:, at : at + z - a], lhsT=dd_codes[:, toks].bitcast(FP8X4), lhsT_scale=dd_scales[:, toks],
-                                    rhs=w3_codes[:, a:z].bitcast(FP8X4), rhs_scale=w3_scales[:, a:z], start=True, stop=True)
+            for w3_cols, bank_cols in ((slice(3 * P, N), slice(0, P)), (slice(0, 2 * P), slice(P, 3 * P))):
+                product(bank[:, bank_cols], dd_codes[:, entries], dd_scales[:, entries],
+                        w3_codes[:, w3_cols], w3_scales[:, w3_cols])
             nc.scalar.activation(turned[:, b, :], bank[:], ACT.Copy, scale=lam_cols[:, b : b + 1])
         back_banks = {}
         for i, t in enumerate(ORDER[1:]):
             back_banks[t] = psum.tile([P, S], F32, name=f"back_bank{t}", tag=f"bank{5 + i}")
-            for b in range(blocks):
+            for b in range(BLOCKS):
                 nc.tensor.transpose(back_banks[t][:, b * P : (b + 1) * P], turned[:, b, i * P : (i + 1) * P], identity[:])
         for t in ORDER[1:]:
             edits[t] = sb(f"edit{t}", [P, S], F32)
             nc.scalar.copy(edits[t][:], back_banks[t][:])
 
         shares = (
-            (nc.vector.tensor_copy, "turned", ((0, 256), (256, 512))),
-            (nc.scalar.copy, "identity", ((512, 768), (768, 896), (896, 1024))),
+            (nc.vector.tensor_copy, "turned", VECTOR_PIECES),
+            (nc.scalar.copy, "identity", SCALAR_PIECES),
         )
-        planes, grouped_out = {}, {}
-        for copy, tag, pieces in shares:
-            a, z = pieces[0][0], pieces[-1][1]
-            planes[a] = sb(f"out_planes{a}", [P, PACK, z - a], BF16, tag)
-            for piece in pieces:
-                grouped_out[piece] = sb(f"out_grouped{piece[0]}", [P, piece[1] - piece[0], PACK], BF16)
+        rounded, woven = {}, {}
+        for tail_copy, tag, pieces in shares:
+            start, end = pieces[0][0], pieces[-1][1]
+            rounded[start] = sb(f"rounded{start}", [P, PACK, end - start], BF16, tag)
+            for a, z in pieces:
+                woven[a, z] = sb(f"woven{a}", [P, z - a, PACK], BF16)
 
-        def round_plane(t, copy, pieces):
-            start = pieces[0][0]
-            for a, z in pieces if t == last else ((start, pieces[-1][1]),):
-                copy(planes[start][:, t, a - start : z - start], windows[t][:, a:z])
+        def round_slot(t, copy, pieces):
+            start, end = pieces[0][0], pieces[-1][1]
+            for a, z in pieces if t == LAST else ((start, end),):
+                copy(rounded[start][:, t, a - start : z - start], windows[t][:, a:z])
 
         def weave_pair(t, copy, pieces):
             start = pieces[0][0]
+            columns = rounded[start][:].rearrange("p t c -> p c t")
             for a, z in pieces:
-                copy(grouped_out[a, z][:, :, t : t + 2], planes[start][:].rearrange("p t c -> p c t")[:, a - start : z - start, t : t + 2])
+                copy(woven[a, z][:, :, t : t + 2], columns[:, a - start : z - start, t : t + 2])
 
         for t in ORDER:
             nc.vector.tensor_tensor(windows[t][:].indirect(offsets[:]), edits[t][:], base_picked[t][:], ALU.add)
-            nc.sync.dma_start(out=out_rows[:, t, :], in_=windows[t][:])
-            for copy, tag, pieces in shares:
-                round_plane(t, copy if t == last else nc.scalar.copy, pieces)
+            nc.sync.dma_start(out=out_slots[:, t, :], in_=windows[t][:])
+            for tail_copy, tag, pieces in shares:
+                round_slot(t, tail_copy if t == LAST else nc.scalar.copy, pieces)
             if t % 2:
-                for copy, tag, pieces in shares:
-                    weave_pair(t - 1, copy if t == last else nc.scalar.copy, pieces)
+                for tail_copy, tag, pieces in shares:
+                    weave_pair(t - 1, tail_copy if t == LAST else nc.scalar.copy, pieces)
 
         out_scales = sb("out_scales", [P, T], U8)
-        word_rows = out_1[0].rearrange("p n r -> p (n r)").bitcast(I32)
         out_codes = sb("out_codes", [P, T], I32)
+        word_rows = out_1[0].rearrange("p n r -> p (n r)").bitcast(I32)
         stored = 0
-        for a, z in grouped_out:
-            nc.vector.quantize_mx(out=out_codes[:, a:z].bitcast(FP8X4), scales=out_scales[:, a:z], in_=grouped_out[a, z][:].rearrange("p c t -> p (c t)"))
-            if z in (512, 768, 1024):
+        for a, z in woven:
+            nc.vector.quantize_mx(
+                out=out_codes[:, a:z].bitcast(FP8X4),
+                scales=out_scales[:, a:z],
+                in_=woven[a, z][:].rearrange("p c t -> p (c t)"),
+            )
+            if z in WORD_STORES:
                 nc.sync.dma_start(out=word_rows[:, stored:z], in_=out_codes[:, stored:z])
                 stored = z
         for q in range(QUADS):
             queue = nc.scalar if q % 2 else nc.sync
-            queue.dma_start(out=out_2[0, 4 * q : 4 * q + 4, :].bitcast(I32), in_=out_scales[32 * q : 32 * q + 4, :].bitcast(I32))
+            queue.dma_start(
+                out=out_2[0, 4 * q : 4 * q + 4, :].bitcast(I32),
+                in_=out_scales[32 * q : 32 * q + 4, :].bitcast(I32),
+            )

from contextlib import ExitStack

import concourse.mybir as mybir
from concourse.masks import make_identity

K, T, S, H, N = 1024, 1024, 512, 512, 512
FLOPS = 2 * S * (2 * K * H + H * N)

F32 = mybir.dt.float32
BF16 = mybir.dt.bfloat16
I32 = mybir.dt.int32
U32 = mybir.dt.uint32
U16 = mybir.dt.uint16
U8 = mybir.dt.uint8
FP8X4 = mybir.dt.float8_e4m3fn_x4
ALU = mybir.AluOpType
ACT = mybir.ActivationFunctionType

P = 128
PACK = 4
K_PASS = P * PACK
QUADS = 4
LIST_ROWS = 16
BLOCKS = S // P

ORDER = (2, 3, 0, 1)
FIRST, LAST = ORDER[0], ORDER[-1]

VECTOR_SHARES = (0, 32, 64, 88)

VECTOR_PIECES = ((0, 256), (256, 512))
SCALAR_PIECES = ((512, 768), (768, 896), (896, 1024))
WORD_STORES = (512, 768, 1024)


def tile_picked_yreft_lin_po_kernel(
    tc, x_words, x_scales, w1, w2, w3, bias, base, lam, offs, out_0, out_1, out_2
):
    nc = tc.nc
    with ExitStack() as ctx:
        keep = ctx.enter_context(tc.tile_pool(name="keep", bufs=1))
        psum = ctx.enter_context(tc.psum_pool(name="psum", bufs=1))

        def sb(name, shape, dtype, tag=None):
            return keep.tile(shape, dtype, name=name, tag=tag or name, align_bytes=64)

        base_slots = base.rearrange("(p t) c -> p t c", t=PACK)
        out_slots = out_0.rearrange("(p t) c -> p t c", t=PACK)

        def load_words(o):
            table = sb(f"word_table{o}", [P, T], I32)
            nc.sync.dma_start(out=table[:], in_=x_words[o].rearrange("p n r -> p (n r)").bitcast(I32))
            return table

        def load_weight(name, rows):
            raw = sb(name, [P, PACK, H], F32)
            nc.sync.dma_start(out=raw[:], in_=rows.rearrange("(p j) c -> p j c", j=PACK))
            return raw

        def load_base(t):
            window = sb(f"window{t}", [P, T], F32)
            nc.sync.dma_start(out=window[:], in_=base_slots[:, t, :])
            return window

        word_tables = [load_words(0)]
        offsets = keep.tile([P, S // LIST_ROWS], U16, name="offsets")
        nc.sync.dma_start(offsets[:], offs)

        scale_table = sb("scale_table", [P, T], U8)
        nc.gpsimd.memset(scale_table[:].bitcast(I32), 0)
        scale_rows = sb("scale_rows", [P, T // 4], I32)
        for q in range(QUADS):
            live = slice(32 * q, 32 * q + 8)
            nc.sync.dma_start(out=scale_rows[live, :], in_=x_scales[:, 4 * q : 4 * q + 4, :].bitcast(I32))
            nc.vector.tensor_copy(scale_table[live, :].bitcast(I32), scale_rows[live, :])

        w12_raw = [load_weight("w1_raw0", w1[0:K_PASS, :])]
        word_tables.append(load_words(1))
        w12_raw.append(load_weight("w1_raw1", w1[K_PASS:K, :]))
        w12_raw.append(load_weight("w2_raw0", w2[0:K_PASS, :]))
        bias_sb = sb("bias_sb", [P, PACK], F32)
        nc.sync.dma_start(out=bias_sb[:], in_=bias.rearrange("(p t) o -> p (t o)", t=PACK))
        w12_raw.append(load_weight("w2_raw1", w2[K_PASS:K, :]))
        windows = {FIRST: load_base(FIRST)}
        w3_raw = load_weight("w3_raw", w3)
        windows[ORDER[1]] = load_base(ORDER[1])
        lam_sb = sb("lam_sb", [P, S], F32)
        nc.sync.dma_start(out=lam_sb[:], in_=lam)
        for t in ORDER[2:]:
            windows[t] = load_base(t)

        def gather_words(o):
            picked = sb(f"x_codes{o}", [P, S], U32)
            nc.vector.tensor_copy(picked[:], word_tables[o][:].bitcast(U32).indirect(offsets[:]))
            return picked

        def gather_base(t, tag=None):
            picked = sb(f"base_picked{t}", [P, S], F32, tag)
            nc.vector.tensor_copy(picked[:], windows[t][:].indirect(offsets[:]))
            return picked

        def round_weight(name, raw, sign, vector_share):
            grouped = sb(name, [P, PACK * H], BF16)
            dealt = grouped[:].rearrange("p (t m j) -> p m t j", t=PACK, j=PACK)
            plain = raw[:].rearrange("p j (m t) -> p m t j", t=PACK)
            if vector_share > 0:
                nc.vector.tensor_scalar(dealt[:, :vector_share], plain[:, :vector_share], sign, None, ALU.mult)
            if vector_share < P:
                nc.scalar.activation(dealt[:, vector_share:], plain[:, vector_share:], ACT.Copy, scale=sign)
            return grouped

        def quantize(name, grouped, calls):
            width = grouped.shape[1] // PACK
            codes = sb(name + "_codes", [P, width], U32)
            scales = sb(name + "_scales", [P, width], U8)
            step = width // calls
            for a in range(0, width, step):
                nc.vector.quantize_mx(
                    out=codes[:, a : a + step].bitcast(FP8X4),
                    scales=scales[:, a : a + step],
                    in_=grouped[:, PACK * a : PACK * (a + step)],
                )
            return codes, scales

        def product(out, left, left_scales, right, right_scales, start=True, stop=True):
            nc.tensor.matmul_mx(
                out=out,
                lhsT=left.bitcast(FP8X4),
                lhsT_scale=left_scales,
                rhs=right.bitcast(FP8X4),
                rhs_scale=right_scales,
                start=start,
                stop=stop,
            )

        x_codes = [gather_words(0)]
        x_scale = sb("x_scale", [P, S], U8)
        nc.vector.tensor_copy(x_scale[:], scale_table[:].indirect(offsets[:]))

        dd_banks = [psum.tile([P, S], F32, name=f"dd_bank{t}", tag=f"bank{t}") for t in range(PACK)]
        passes = [(sign, o) for sign in (1.0, -1.0) for o in range(K // K_PASS)]
        for i, (sign, o) in enumerate(passes):
            closing = i == len(passes) - 1
            grouped = round_weight(f"w12_grouped{i}", w12_raw[i], sign, VECTOR_SHARES[i])
            codes, scales = quantize(f"w12_{i}", grouped, 2 if closing else 1)
            if i == 0:
                x_codes.append(gather_words(1))
            for t in range(PACK):
                slot = slice(t * P, (t + 1) * P)
                product(dd_banks[t][:], codes[:, slot], scales[:, slot], x_codes[o][:], x_scale[4 * o : P, :],
                        start=(i == 0), stop=closing)

        identity = sb("identity", [P, P], F32)
        make_identity(nc, identity[:])
        lam_bank = psum.tile([P, BLOCKS, P], F32, name="lam_bank", tag="bank5")
        for b in range(BLOCKS):
            nc.tensor.transpose(lam_bank[:, b, :], lam_sb[:, b * P : (b + 1) * P], identity[:])
        lam_cols = sb("lam_cols", [P, BLOCKS], F32)

        dd_slots = sb("dd_slots", [P, PACK, S], BF16)
        base_picked = {FIRST: gather_base(FIRST)}
        for t in range(PACK - 1):
            nc.scalar.activation(dd_slots[:, t, :], dd_banks[t][:], ACT.Identity, bias=bias_sb[:, t : t + 1])
        nc.vector.tensor_scalar(dd_slots[:, PACK - 1, :], dd_banks[PACK - 1][:], bias_sb[:, PACK - 1 :], None, ALU.add)
        w3_grouped = round_weight("w3_grouped", w3_raw, 1.0, P)
        base_picked[ORDER[1]] = gather_base(ORDER[1])
        w3_codes, w3_scales = quantize("w3", w3_grouped, 1)
        dd_grouped = sb("dd_grouped", [P, PACK * S], BF16)
        nc.scalar.copy(
            dd_grouped[:].rearrange("p (c i t) -> p c t i", i=4, t=PACK),
            dd_slots[:].rearrange("p t (c i) -> p c t i", i=4),
        )
        nc.scalar.copy(lam_cols[:], lam_bank[:, :, 0])
        dd_codes, dd_scales = quantize("dd", dd_grouped, 1)
        base_picked[ORDER[2]] = gather_base(ORDER[2], "dd_grouped")

        edits = {FIRST: sb("edit_first", [P, S], F32)}
        ed_bank = psum.tile([P, S], F32, name="ed_bank", tag="bank4")
        slot = slice(FIRST * P, (FIRST + 1) * P)
        product(ed_bank[:], w3_codes[:, slot], w3_scales[:, slot], dd_codes[:], dd_scales[:])
        nc.vector.tensor_tensor(edits[FIRST][:], ed_bank[:], lam_sb[:], ALU.mult)
        base_picked[LAST] = gather_base(LAST)

        turned = sb("turned", [P, BLOCKS, N - P], F32)
        for b in range(BLOCKS):
            entries = slice(b * P, (b + 1) * P)
            bank = psum.tile([P, N - P], F32, name=f"turned_bank{b}", tag=f"bank{b}")
            for w3_cols, bank_cols in ((slice(3 * P, N), slice(0, P)), (slice(0, 2 * P), slice(P, 3 * P))):
                product(bank[:, bank_cols], dd_codes[:, entries], dd_scales[:, entries],
                        w3_codes[:, w3_cols], w3_scales[:, w3_cols])
            nc.scalar.activation(turned[:, b, :], bank[:], ACT.Copy, scale=lam_cols[:, b : b + 1])
        back_banks = {}
        for i, t in enumerate(ORDER[1:]):
            back_banks[t] = psum.tile([P, S], F32, name=f"back_bank{t}", tag=f"bank{5 + i}")
            for b in range(BLOCKS):
                nc.tensor.transpose(back_banks[t][:, b * P : (b + 1) * P], turned[:, b, i * P : (i + 1) * P], identity[:])
        for t in ORDER[1:]:
            edits[t] = sb(f"edit{t}", [P, S], F32)
            nc.scalar.copy(edits[t][:], back_banks[t][:])

        shares = (
            (nc.vector.tensor_copy, "turned", VECTOR_PIECES),
            (nc.scalar.copy, "identity", SCALAR_PIECES),
        )
        rounded, woven = {}, {}
        for tail_copy, tag, pieces in shares:
            start, end = pieces[0][0], pieces[-1][1]
            rounded[start] = sb(f"rounded{start}", [P, PACK, end - start], BF16, tag)
            for a, z in pieces:
                woven[a, z] = sb(f"woven{a}", [P, z - a, PACK], BF16)

        def round_slot(t, copy, pieces):
            start, end = pieces[0][0], pieces[-1][1]
            for a, z in pieces if t == LAST else ((start, end),):
                copy(rounded[start][:, t, a - start : z - start], windows[t][:, a:z])

        def weave_pair(t, copy, pieces):
            start = pieces[0][0]
            columns = rounded[start][:].rearrange("p t c -> p c t")
            for a, z in pieces:
                copy(woven[a, z][:, :, t : t + 2], columns[:, a - start : z - start, t : t + 2])

        for t in ORDER:
            nc.vector.tensor_tensor(windows[t][:].indirect(offsets[:]), edits[t][:], base_picked[t][:], ALU.add)
            nc.sync.dma_start(out=out_slots[:, t, :], in_=windows[t][:])
            for tail_copy, tag, pieces in shares:
                round_slot(t, tail_copy if t == LAST else nc.scalar.copy, pieces)
            if t % 2:
                for tail_copy, tag, pieces in shares:
                    weave_pair(t - 1, tail_copy if t == LAST else nc.scalar.copy, pieces)

        out_scales = sb("out_scales", [P, T], U8)
        out_codes = sb("out_codes", [P, T], I32)
        word_rows = out_1[0].rearrange("p n r -> p (n r)").bitcast(I32)
        stored = 0
        for a, z in woven:
            nc.vector.quantize_mx(
                out=out_codes[:, a:z].bitcast(FP8X4),
                scales=out_scales[:, a:z],
                in_=woven[a, z][:].rearrange("p c t -> p (c t)"),
            )
            if z in WORD_STORES:
                nc.sync.dma_start(out=word_rows[:, stored:z], in_=out_codes[:, stored:z])
                stored = z
        for q in range(QUADS):
            queue = nc.scalar if q % 2 else nc.sync
            queue.dma_start(
                out=out_2[0, 4 * q : 4 * q + 4, :].bitcast(I32),
                in_=out_scales[32 * q : 32 * q + 4, :].bitcast(I32),
            )
